import numpy as np
import ml_dtypes


def mxq(x, axis, fmt="e4m3"):
    dtype, down = {"e4m3": (ml_dtypes.float8_e4m3fn, 7), "e5m2": (ml_dtypes.float8_e5m2, 14)}[fmt]
    v = np.moveaxis(np.asarray(x, np.float32).astype(ml_dtypes.bfloat16).astype(np.float64), axis, -1)
    blocks = v.reshape(v.shape[:-1] + (-1, 32))
    amax = np.abs(blocks).max(-1, keepdims=True)
    byte = np.maximum(np.where(amax > 0, np.frexp(amax)[1] - 1 + 127, 0) - down, 1)
    scale = np.exp2(byte - 127.0)
    codes = (blocks / scale).astype(np.float32).astype(dtype).astype(np.float64)
    return np.moveaxis((codes * scale).reshape(v.shape), -1, axis)


WIDE = False


def mx_kscale(k):
    if not WIDE:
        return np.ones(k)
    levels = np.array([10, -10, 5, -5, 0])
    if k % 512:
        return np.exp2(np.random.permutation(np.resize(levels, k // 32))).repeat(32)
    a = np.empty((k // 512, 16))
    for p in range(k // 512):
        a[p, :8] = np.random.permutation(np.resize(levels, 8))
        for g in range(8):
            far = levels[np.abs(levels - a[p, g]) >= 10]
            a[p, g + 8] = far[np.random.randint(len(far))]
    return np.exp2(a.ravel()).repeat(32)


def f64(x):
    return np.asarray(x).astype(np.float64)


def striped(idx):
    return np.tile(idx.reshape(-1, 16).T, (8, 1)).astype(np.uint16)


def unstriped(offs):
    return offs[:16].T.reshape(-1).astype(np.int64)


def striped8(idx):
    return np.concatenate([x.reshape(-1, 16).T for x in idx]).astype(np.uint16)


def runs(offs, k):
    lists = np.stack([offs[16 * r : 16 * r + 16].T.reshape(-1) for r in range(8)]).astype(np.int64)
    return lists[np.arange(k) % 512 // 64]


def pack_weight(w):
    k, n = w.shape
    w = f64(np.asarray(w, np.float32).astype(ml_dtypes.bfloat16)).reshape(k // 32, 32, n)
    amax = np.abs(w).max(1)
    byte = np.clip(np.where(amax > 0, np.frexp(amax)[1] - 1 + 127 - 7, 1), 1, 254)
    scaled = (w * np.exp2(127.0 - byte)[:, None, :]).reshape(k, n).astype(np.float32)
    words = np.ascontiguousarray(scaled.reshape(k // 512, 128, 4, n).transpose(0, 1, 3, 2)).astype(ml_dtypes.float8_e4m3fn).view(np.uint8)
    return words, np.ascontiguousarray(byte.astype(np.uint8).reshape(k // 512, 16, n))


def unpack_weight(words, scales):
    g, p, n, _ = words.shape
    vals = np.ascontiguousarray(words).view(ml_dtypes.float8_e4m3fn).astype(np.float64) * np.repeat(np.exp2(scales.astype(np.float64) - 127.0), 8, axis=1)[..., None]
    return vals.transpose(0, 1, 3, 2).reshape(g * 512, n)


K, T, S, N, H, C = 512, 2048, 256, 512, 512, 512


def setup_inputs():
    n = np.random.standard_normal
    s = mx_kscale(K)[:, None]
    u = mx_kscale(K)
    packed_xT = pack_weight(n((K, T)) * s)
    return {
        "x_words": packed_xT[0],
        "x_scales": packed_xT[1],
        "w1": (n((K, H)) / np.sqrt(K) / s).astype(np.float32),
        "gn": (np.random.uniform(0.5, 1.5, (H, 1)) * u[:, None]).astype(np.float32),
        "w2": (n((H, N)) / np.sqrt(H) / u[:, None]).astype(np.float32),
        "gs": (np.random.uniform(0.5, 1.5, (K, 1)) / s).astype(np.float32),
        "offs": striped(np.random.permutation(T)[:S]),
        "n1": striped(np.random.permutation(S)),
        "n2": striped(np.random.permutation(S)),
        "n3": striped8(np.stack([np.random.permutation(S) for _ in range(8)])),
        "n4": striped8(np.stack([np.random.permutation(S) for _ in range(8)])),
        "n5": striped8(np.stack([np.random.permutation(S) for _ in range(8)])),
        "cand": striped(np.random.permutation(T)[:C]),
        "n6": striped(np.random.permutation(S)),
        "n7": striped(np.random.permutation(S)),
    }


def reference(x_words, x_scales, w1, gn, w2, gs, offs, n1, n2, n3, n4, n5, cand, n6, n7):
    xq = unpack_weight(x_words, x_scales)[:, unstriped(offs)]
    y = mxq(f64(w1), 0, "e4m3").T @ xq
    pa = y[:, unstriped(n1)]
    pb = y[:, unstriped(n2)]
    mu = 0.3125 * (y + pa + pb)
    z = f64(gn) * ((y - mu) / (np.sqrt((pa - mu) ** 2 + (pb - mu) ** 2 + 0.25)))
    a = mxq(f64(w2), 0, "e4m3").T @ mxq(z, 0, "e4m3")
    x_cand = unpack_weight(x_words, x_scales)[:, unstriped(cand)]
    z2 = f64(gs) * (np.maximum(y, y[np.arange(H)[:, None], runs(n3, H)]) - (np.maximum(y[np.arange(H)[:, None], runs(n4, H)], y[np.arange(H)[:, None], runs(n5, H)])))
    b = 0.0625 * ((x_cand.T @ mxq(z2, 0, "e4m3")))
    return a * (np.tanh(b[:, unstriped(n6)] - b[:, unstriped(n7)]))

@@ -1,0 +1,195 @@
+from contextlib import ExitStack
+
+import concourse.mybir as mybir
+
+K, T, S, N, H, C = 512, 2048, 256, 512, 512, 512
+FLOPS = 2 * K * H * S + 2 * H * N * S + 2 * K * C * S
+
+F32 = mybir.dt.float32
+BF16 = mybir.dt.bfloat16
+I32 = mybir.dt.int32
+U32 = mybir.dt.uint32
+U16 = mybir.dt.uint16
+U8 = mybir.dt.uint8
+FP8X4 = mybir.dt.float8_e4m3fn_x4
+ALU = mybir.AluOpType
+ACT = mybir.ActivationFunctionType
+
+P = 128
+PACK = 4
+WINDOW = 2 * S
+
+
+def tile_picked_fkcdjointbstdmix_none_p_kernel(
+    tc, x_words, x_scales, w1, gn, w2, gs, offs, n1, n2, n3, n4, n5, cand, n6, n7, out
+):
+    nc = tc.nc
+    with ExitStack() as ctx:
+        keep = ctx.enter_context(tc.tile_pool(name="keep", bufs=1))
+        psum = ctx.enter_context(tc.psum_pool(name="psum", bufs=1))
+
+        def load_list(name, src):
+            tile = keep.tile(list(src.shape), U16, name=name)
+            nc.sync.dma_start(tile[:], src)
+            return tile
+
+        def mx(dst, lhs_codes, lhs_scales, rhs_codes, rhs_scales):
+            nc.tensor.matmul_mx(
+                out=dst,
+                lhsT=lhs_codes.bitcast(FP8X4),
+                lhsT_scale=lhs_scales,
+                rhs=rhs_codes.bitcast(FP8X4),
+                rhs_scale=rhs_scales,
+                start=True,
+                stop=True,
+            )
+
+        x_scale_table = keep.tile([P, T], U8, align_bytes=64)
+        nc.vector.memset(x_scale_table[:].bitcast(I32), 0)
+        offs_t = load_list("offs_t", offs)
+        w1_raw = keep.tile([P, PACK, H], F32)
+        nc.sync.dma_start(w1_raw[:], w1.rearrange("(p j) c -> p j c", j=PACK))
+        for q in range(4):
+            nc.scalar.dma_start(
+                x_scale_table[32 * q : 32 * q + 4, :].bitcast(I32),
+                x_scales[0, 4 * q : 4 * q + 4, :].bitcast(I32),
+            )
+        cand_t = load_list("cand_t", cand)
+        x_word_table = keep.tile([P, T], U32, align_bytes=64)
+        nc.sync.dma_start(
+            x_word_table[:].bitcast(I32), x_words[0].rearrange("p n r -> p (n r)").bitcast(I32)
+        )
+        n1_t = load_list("n1_t", n1)
+        n2_t = load_list("n2_t", n2)
+        n3_t = load_list("n3_t", n3)
+        n4_t = load_list("n4_t", n4)
+        n5_t = load_list("n5_t", n5)
+        w2_raw = keep.tile([P, PACK, N], F32)
+        nc.sync.dma_start(w2_raw[:], w2.rearrange("(p j) c -> p j c", j=PACK))
+        n6_t = load_list("n6_t", n6)
+        n7_t = load_list("n7_t", n7)
+        gn_t = keep.tile([P, PACK], F32)
+        nc.gpsimd.dma_start(gn_t[:], gn.rearrange("(p t) o -> p (t o)", t=PACK))
+        gs_t = keep.tile([P, PACK], F32)
+        nc.gpsimd.dma_start(gs_t[:], gs.rearrange("(p t) o -> p (t o)", t=PACK))
+
+        y_rows = [keep.tile([P, WINDOW], F32, name="y_rows%d" % t) for t in range(PACK)]
+        b_rows = [keep.tile([P, WINDOW], F32, name="b_rows%d" % t) for t in range(PACK)]
+        for rows in y_rows + b_rows:
+            nc.gpsimd.memset(rows[:, S:], 0.0)
+
+        pick_scales = keep.tile([P, S], U8, align_bytes=64)
+        nc.vector.tensor_copy(pick_scales[:], x_scale_table[:].indirect(offs_t[:]))
+        cand_scales = keep.tile([P, C], U8, align_bytes=64)
+        nc.vector.tensor_copy(cand_scales[:], x_scale_table[:].indirect(cand_t[:]))
+        w1_bf = keep.tile([P, PACK, P, PACK], BF16, align_bytes=64)
+        nc.vector.tensor_copy(
+            w1_bf[:].rearrange("p t m j -> p m j t"), w1_raw[:].rearrange("p j (m t) -> p m j t", t=PACK)
+        )
+        w1_codes = keep.tile([P, H], U32, align_bytes=64)
+        w1_scales = keep.tile([P, H], U8, align_bytes=64)
+        nc.vector.quantize_mx(w1_codes[:].bitcast(FP8X4), w1_scales[:], w1_bf[:].rearrange("p t m j -> p (t m j)"))
+        pick_words = keep.tile([P, S], U32, align_bytes=64)
+        nc.vector.tensor_copy(pick_words[:], x_word_table[:].indirect(offs_t[:]))
+
+        y_psum = [psum.tile([P, S], F32, name="y_psum%d" % t) for t in range(PACK)]
+        for t in range(PACK):
+            cols = slice(P * t, P * (t + 1))
+            mx(y_psum[t][:], w1_codes[:, cols], w1_scales[:, cols], pick_words[:], pick_scales[:])
+        for t in range(PACK):
+            nc.vector.tensor_copy(y_rows[t][:, :S], y_psum[t][:])
+
+        pa = keep.tile([P, PACK, S], F32)
+        for t in range(PACK):
+            nc.scalar.activation(pa[:, t, :], y_rows[t][:].indirect(n1_t[:]), ACT.Copy)
+        y3 = keep.tile([P, PACK, S], F32)
+        y4 = keep.tile([P, PACK, S], F32)
+        y5 = keep.tile([P, PACK, S], F32)
+        for t in range(PACK):
+            nc.scalar.activation(y3[:, t, :], y_rows[t][:].indirect(n3_t[:]), ACT.Copy)
+            nc.scalar.activation(y4[:, t, :], y_rows[t][:].indirect(n4_t[:]), ACT.Copy)
+            nc.scalar.activation(y5[:, t, :], y_rows[t][:].indirect(n5_t[:]), ACT.Copy)
+
+        u = keep.tile([P, PACK, S], F32)
+        for t in range(PACK):
+            nc.vector.tensor_tensor(u[:, t, :], y_rows[t][:].indirect(n2_t[:]), pa[:, t, :], ALU.add)
+        ev = keep.tile([P, 2, PACK, S], F32)
+        centred = keep.tile([P, PACK, S], F32)
+        for t in range(PACK):
+            nc.vector.scalar_tensor_tensor(ev[:, 0, t, :], y_rows[t][:, :S], -5.0 / 3.0, u[:, t, :], ALU.mult, ALU.add)
+        nc.vector.scalar_tensor_tensor(ev[:, 1, :, :], pa[:], -2.0, u[:], ALU.mult, ALU.add)
+        for t in range(PACK):
+            nc.vector.scalar_tensor_tensor(centred[:, t, :], y_rows[t][:, :S], 2.2, u[:, t, :], ALU.mult, ALU.subtract)
+
+        cand_words = keep.tile([P, C], U32, align_bytes=64)
+        nc.vector.tensor_copy(cand_words[:], x_word_table[:].indirect(cand_t[:]))
+        w2_bf = keep.tile([P, N, PACK], BF16, align_bytes=64)
+        nc.vector.tensor_copy(
+            w2_bf[:].rearrange("p (c i) j -> p c j i", i=4), w2_raw[:].rearrange("p j (c i) -> p c j i", i=4)
+        )
+
+        max_a = keep.tile([P, PACK, S], F32)
+        max_b = keep.tile([P, PACK, S], F32)
+        diff = keep.tile([P, PACK, S], F32)
+        for t in range(PACK):
+            nc.vector.tensor_tensor(max_a[:, t, :], y3[:, t, :], y_rows[t][:, :S], ALU.max)
+            nc.vector.tensor_tensor(max_b[:, t, :], y4[:, t, :], y5[:, t, :], ALU.max)
+        w2_codes = keep.tile([P, N], U32, align_bytes=64)
+        w2_scales = keep.tile([P, N], U8, align_bytes=64)
+        nc.vector.quantize_mx(w2_codes[:].bitcast(FP8X4), w2_scales[:], w2_bf[:].rearrange("p c j -> p (c j)"))
+        nc.vector.tensor_tensor(diff[:], max_a[:], max_b[:], ALU.subtract)
+
+        squares = keep.tile([P, 2, PACK, S], F32)
+        nc.scalar.activation(squares[:], ev[:], ACT.Square)
+
+        z2_bf = keep.tile([P, S, PACK], BF16, align_bytes=64)
+        nc.vector.tensor_tensor(
+            z2_bf[:].rearrange("p (c i) t -> p c t i", i=4),
+            diff[:].rearrange("p t (c i) -> p c t i", i=4),
+            gs_t[:].unsqueeze(1).unsqueeze(3).broadcast_to([P, S // 4, PACK, 4]),
+            ALU.mult,
+        )
+        spread = keep.tile([P, PACK, S], F32)
+        nc.vector.scalar_tensor_tensor(spread[:], squares[:, 0, :, :], 0.140625, squares[:, 1, :, :], ALU.mult, ALU.add)
+        z2_codes = keep.tile([P, S], U32, align_bytes=64)
+        z2_scales = keep.tile([P, S], U8, align_bytes=64)
+        nc.vector.quantize_mx(z2_codes[:].bitcast(FP8X4), z2_scales[:], z2_bf[:].rearrange("p j t -> p (j t)"))
+
+        inv = keep.tile([P, PACK, S], F32)
+        nc.scalar.activation(inv[:], spread[:], ACT.Abs_reciprocal_sqrt, bias=2.56, scale=5.12)
+
+        b_psum = [psum.tile([P, 2, S], F32, name="b_psum%d" % h) for h in range(2)]
+        for r in range(4):
+            cols = slice(P * r, P * (r + 1))
+            mx(b_psum[r // 2][:, r % 2, :], cand_words[:, cols], cand_scales[:, cols], z2_codes[:], z2_scales[:])
+        b6 = keep.tile([P, 4, S], F32)
+        for r in range(4):
+            nc.scalar.copy(b_rows[r][:, :S], b_psum[r // 2][:, r % 2, :])
+            nc.scalar.activation(b6[:, r, :], b_rows[r][:].indirect(n6_t[:]), ACT.Copy)
+
+        z = keep.tile([P, PACK, S], F32)
+        for t in range(PACK):
+            nc.vector.scalar_tensor_tensor(z[:, t, :], centred[:, t, :], gn_t[:, t : t + 1], inv[:, t, :], ALU.mult, ALU.mult)
+        z_bf = keep.tile([P, S, PACK], BF16, align_bytes=64)
+        nc.vector.tensor_copy(
+            z_bf[:].rearrange("p (c i) t -> p c t i", i=4), z[:].rearrange("p t (c i) -> p c t i", i=4)
+        )
+        b_diff = keep.tile([P, 4, S], F32)
+        nc.vector.tensor_tensor(b_diff[:, 0, :], b_rows[0][:].indirect(n7_t[:]), b6[:, 0, :], ALU.subtract)
+        z_codes = keep.tile([P, S], U32, align_bytes=64)
+        z_scales = keep.tile([P, S], U8, align_bytes=64)
+        nc.vector.quantize_mx(z_codes[:].bitcast(FP8X4), z_scales[:], z_bf[:].rearrange("p j t -> p (j t)"))
+        a_psum = [psum.tile([P, 2, S], F32, name="a_psum%d" % h) for h in range(2)]
+        for r in range(4):
+            cols = slice(P * r, P * (r + 1))
+            mx(a_psum[r // 2][:, r % 2, :], w2_codes[:, cols], w2_scales[:, cols], z_codes[:], z_scales[:])
+        for r in range(1, 4):
+            nc.vector.tensor_tensor(b_diff[:, r, :], b_rows[r][:].indirect(n7_t[:]), b6[:, r, :], ALU.subtract)
+
+        gate = keep.tile([P, 4, S], F32)
+        result = keep.tile([P, 4, S], F32)
+        for r in range(4):
+            nc.scalar.activation(gate[:, r, :], b_diff[:, r, :], ACT.Tanh, scale=-0.0625)
+        for r in range(4):
+            nc.vector.tensor_tensor(result[:, r, :], a_psum[r // 2][:, r % 2, :], gate[:, r, :], ALU.mult)
+            nc.sync.dma_start(out[P * r : P * (r + 1), :], result[:, r, :])

@@ -1,6 +1,7 @@
 from contextlib import ExitStack
 
 import concourse.mybir as mybir
+from concourse.masks import make_identity
 
 K, T, S, N, H, C = 512, 2048, 256, 512, 512, 512
 FLOPS = 2 * K * H * S + 2 * H * N * S + 2 * K * C * S
@@ -17,7 +18,13 @@ ACT = mybir.ActivationFunctionType
 
 P = 128
 PACK = 4
+BLOCKS = N // P
+HALVES = S // P
 WINDOW = 2 * S
+RUN = 4
+
+ROOT_SCALE = 0.5 / 0.3125**2
+ROOT_BIAS = 0.25 / 0.3125**2
 
 
 def tile_picked_fkcdjointbstdmix_none_p_kernel(
@@ -28,168 +35,237 @@ def tile_picked_fkcdjointbstdmix_none_p_kernel(
         keep = ctx.enter_context(tc.tile_pool(name="keep", bufs=1))
         psum = ctx.enter_context(tc.psum_pool(name="psum", bufs=1))
 
-        def load_list(name, src):
-            tile = keep.tile(list(src.shape), U16, name=name)
-            nc.sync.dma_start(tile[:], src)
+        def load_list(name, source):
+            tile = keep.tile(list(source.shape), U16, name=name)
+            nc.sync.dma_start(tile[:], source)
             return tile
 
-        def mx(dst, lhs_codes, lhs_scales, rhs_codes, rhs_scales):
+        def four_tiles(name):
+            return keep.tile([P, PACK, S], F32, name=name)
+
+        def mx_operand(name, columns):
+            words = keep.tile([P, columns], U32, name=name + "_words", align_bytes=64)
+            scales = keep.tile([P, columns], U8, name=name + "_scales", align_bytes=64)
+            return words, scales
+
+        def interleave(grouped, tiles):
+            nc.vector.tensor_copy(
+                grouped[:].rearrange("p (c i) t -> p c t i", i=RUN),
+                tiles[:].rearrange("p t (c i) -> p c t i", i=RUN),
+            )
+
+        def quantize(words, scales, grouped):
+            nc.vector.quantize_mx(words.bitcast(FP8X4), scales, grouped)
+
+        def product(result, block, stationary, moving):
+            columns = slice(P * block, P * (block + 1))
             nc.tensor.matmul_mx(
-                out=dst,
-                lhsT=lhs_codes.bitcast(FP8X4),
-                lhsT_scale=lhs_scales,
-                rhs=rhs_codes.bitcast(FP8X4),
-                rhs_scale=rhs_scales,
+                out=result,
+                lhsT=stationary[0][:, columns].bitcast(FP8X4),
+                lhsT_scale=stationary[1][:, columns],
+                rhs=moving[0][:].bitcast(FP8X4),
+                rhs_scale=moving[1][:],
                 start=True,
                 stop=True,
             )
 
-        x_scale_table = keep.tile([P, T], U8, align_bytes=64)
-        nc.vector.memset(x_scale_table[:].bitcast(I32), 0)
-        offs_t = load_list("offs_t", offs)
-        w1_raw = keep.tile([P, PACK, H], F32)
-        nc.sync.dma_start(w1_raw[:], w1.rearrange("(p j) c -> p j c", j=PACK))
-        for q in range(4):
-            nc.scalar.dma_start(
-                x_scale_table[32 * q : 32 * q + 4, :].bitcast(I32),
-                x_scales[0, 4 * q : 4 * q + 4, :].bitcast(I32),
-            )
-        cand_t = load_list("cand_t", cand)
-        x_word_table = keep.tile([P, T], U32, align_bytes=64)
-        nc.sync.dma_start(
-            x_word_table[:].bitcast(I32), x_words[0].rearrange("p n r -> p (n r)").bitcast(I32)
-        )
-        n1_t = load_list("n1_t", n1)
-        n2_t = load_list("n2_t", n2)
-        n3_t = load_list("n3_t", n3)
-        n4_t = load_list("n4_t", n4)
-        n5_t = load_list("n5_t", n5)
-        w2_raw = keep.tile([P, PACK, N], F32)
-        nc.sync.dma_start(w2_raw[:], w2.rearrange("(p j) c -> p j c", j=PACK))
-        n6_t = load_list("n6_t", n6)
-        n7_t = load_list("n7_t", n7)
-        gn_t = keep.tile([P, PACK], F32)
-        nc.gpsimd.dma_start(gn_t[:], gn.rearrange("(p t) o -> p (t o)", t=PACK))
-        gs_t = keep.tile([P, PACK], F32)
-        nc.gpsimd.dma_start(gs_t[:], gs.rearrange("(p t) o -> p (t o)", t=PACK))
+        def transposed_sum(result, terms):
+            for i, term in enumerate(terms):
+                nc.tensor.matmul(
+                    result, term, identity[:], start=(i == 0), stop=(i == len(terms) - 1), is_transpose=True
+                )
 
+        def fetch(result, rows, offsets, scale=1.0):
+            nc.scalar.activation(result, rows[:].indirect(offsets[:]), ACT.Copy, scale=scale)
+
+        identity = keep.tile([P, P], F32)
+        make_identity(nc, identity[:])
+
+        gs_tile = keep.tile([P, PACK], F32)
+        nc.gpsimd.dma_start(gs_tile[:], gs.rearrange("(p t) o -> p (t o)", t=PACK))
+        gn_tile = keep.tile([P, PACK], F32)
+        nc.gpsimd.dma_start(gn_tile[:], gn.rearrange("(p t) o -> p (t o)", t=PACK))
+
+        scale_table = keep.tile([P, T], U8, align_bytes=64)
+        nc.vector.memset(scale_table[:].bitcast(I32), 0)
         y_rows = [keep.tile([P, WINDOW], F32, name="y_rows%d" % t) for t in range(PACK)]
-        b_rows = [keep.tile([P, WINDOW], F32, name="b_rows%d" % t) for t in range(PACK)]
+        b_rows = [keep.tile([P, WINDOW], F32, name="b_rows%d" % r) for r in range(BLOCKS)]
         for rows in y_rows + b_rows:
-            nc.gpsimd.memset(rows[:, S:], 0.0)
+            nc.vector.memset(rows[:, S:], 0.0)
 
-        pick_scales = keep.tile([P, S], U8, align_bytes=64)
-        nc.vector.tensor_copy(pick_scales[:], x_scale_table[:].indirect(offs_t[:]))
-        cand_scales = keep.tile([P, C], U8, align_bytes=64)
-        nc.vector.tensor_copy(cand_scales[:], x_scale_table[:].indirect(cand_t[:]))
-        w1_bf = keep.tile([P, PACK, P, PACK], BF16, align_bytes=64)
-        nc.vector.tensor_copy(
-            w1_bf[:].rearrange("p t m j -> p m j t"), w1_raw[:].rearrange("p j (m t) -> p m j t", t=PACK)
-        )
-        w1_codes = keep.tile([P, H], U32, align_bytes=64)
-        w1_scales = keep.tile([P, H], U8, align_bytes=64)
-        nc.vector.quantize_mx(w1_codes[:].bitcast(FP8X4), w1_scales[:], w1_bf[:].rearrange("p t m j -> p (t m j)"))
-        pick_words = keep.tile([P, S], U32, align_bytes=64)
-        nc.vector.tensor_copy(pick_words[:], x_word_table[:].indirect(offs_t[:]))
-
-        y_psum = [psum.tile([P, S], F32, name="y_psum%d" % t) for t in range(PACK)]
-        for t in range(PACK):
-            cols = slice(P * t, P * (t + 1))
-            mx(y_psum[t][:], w1_codes[:, cols], w1_scales[:, cols], pick_words[:], pick_scales[:])
-        for t in range(PACK):
-            nc.vector.tensor_copy(y_rows[t][:, :S], y_psum[t][:])
-
-        pa = keep.tile([P, PACK, S], F32)
-        for t in range(PACK):
-            nc.scalar.activation(pa[:, t, :], y_rows[t][:].indirect(n1_t[:]), ACT.Copy)
-        y3 = keep.tile([P, PACK, S], F32)
-        y4 = keep.tile([P, PACK, S], F32)
-        y5 = keep.tile([P, PACK, S], F32)
-        for t in range(PACK):
-            nc.scalar.activation(y3[:, t, :], y_rows[t][:].indirect(n3_t[:]), ACT.Copy)
-            nc.scalar.activation(y4[:, t, :], y_rows[t][:].indirect(n4_t[:]), ACT.Copy)
-            nc.scalar.activation(y5[:, t, :], y_rows[t][:].indirect(n5_t[:]), ACT.Copy)
-
-        u = keep.tile([P, PACK, S], F32)
-        for t in range(PACK):
-            nc.vector.tensor_tensor(u[:, t, :], y_rows[t][:].indirect(n2_t[:]), pa[:, t, :], ALU.add)
-        ev = keep.tile([P, 2, PACK, S], F32)
-        centred = keep.tile([P, PACK, S], F32)
-        for t in range(PACK):
-            nc.vector.scalar_tensor_tensor(ev[:, 0, t, :], y_rows[t][:, :S], -5.0 / 3.0, u[:, t, :], ALU.mult, ALU.add)
-        nc.vector.scalar_tensor_tensor(ev[:, 1, :, :], pa[:], -2.0, u[:], ALU.mult, ALU.add)
-        for t in range(PACK):
-            nc.vector.scalar_tensor_tensor(centred[:, t, :], y_rows[t][:, :S], 2.2, u[:, t, :], ALU.mult, ALU.subtract)
-
-        cand_words = keep.tile([P, C], U32, align_bytes=64)
-        nc.vector.tensor_copy(cand_words[:], x_word_table[:].indirect(cand_t[:]))
-        w2_bf = keep.tile([P, N, PACK], BF16, align_bytes=64)
-        nc.vector.tensor_copy(
-            w2_bf[:].rearrange("p (c i) j -> p c j i", i=4), w2_raw[:].rearrange("p j (c i) -> p c j i", i=4)
+        warm_root = keep.tile([P, 1], F32)
+        nc.scalar.activation(
+            warm_root[:], y_rows[0][:, S : S + 1], ACT.Abs_reciprocal_sqrt, bias=ROOT_BIAS, scale=ROOT_SCALE
         )
 
-        max_a = keep.tile([P, PACK, S], F32)
-        max_b = keep.tile([P, PACK, S], F32)
-        diff = keep.tile([P, PACK, S], F32)
+        offs_tile = load_list("offs_tile", offs)
+        cand_tile = load_list("cand_tile", cand)
+        w1_rows = w1.rearrange("(p j) c -> p j c", j=PACK)
+        w1_low = keep.tile([P, PACK, H // 2], F32)
+        nc.sync.dma_start(w1_low[:], w1_rows[:, :, : H // 2])
+        for quadrant in range(4):
+            nc.sync.dma_start(
+                scale_table[32 * quadrant : 32 * quadrant + 4, :].bitcast(I32),
+                x_scales[0, 4 * quadrant : 4 * quadrant + 4, :].bitcast(I32),
+            )
+        w1_high = keep.tile([P, PACK, H // 2], F32)
+        nc.sync.dma_start(w1_high[:], w1_rows[:, :, H // 2 :])
+        word_table = keep.tile([P, T], U32, align_bytes=64)
+        nc.sync.dma_start(word_table[:].bitcast(I32), x_words[0].rearrange("p c r -> p (c r)").bitcast(I32))
+        n1_tile = load_list("n1_tile", n1)
+        n2_tile = load_list("n2_tile", n2)
+        n4_tile = load_list("n4_tile", n4)
+        n5_tile = load_list("n5_tile", n5)
+        n3_tile = load_list("n3_tile", n3)
+        w2_rows = keep.tile([P, PACK, N], F32)
+        nc.sync.dma_start(w2_rows[:], w2.rearrange("(p j) c -> p j c", j=PACK))
+        n6_tile = load_list("n6_tile", n6)
+        n7_tile = load_list("n7_tile", n7)
+
+        picked = mx_operand("picked", S)
+        candidates = mx_operand("candidates", C)
+        w1_mx = mx_operand("w1_mx", H)
+        w1_grouped = keep.tile([P, PACK, P, PACK], BF16, align_bytes=64)
+
+        def dealt(first, last):
+            return w1_grouped[:, :, first:last, :].rearrange("p t m j -> p m j t")
+
+        def by_channel(columns):
+            return columns.rearrange("p j (m t) -> p m j t", t=PACK)
+
+        nc.scalar.activation(dealt(0, P // 2), by_channel(w1_low[:]), ACT.Copy)
+        nc.vector.tensor_copy(picked[1][:], scale_table[:].indirect(offs_tile[:]))
+        nc.vector.tensor_copy(candidates[1][:], scale_table[:].indirect(cand_tile[:]))
+        nc.vector.tensor_copy(dealt(P // 2, 3 * P // 4), by_channel(w1_high[:, :, : H // 4]))
+        nc.scalar.activation(dealt(3 * P // 4, P), by_channel(w1_high[:, :, H // 4 :]), ACT.Copy)
+        for pair in range(PACK // 2):
+            columns = slice(2 * P * pair, 2 * P * (pair + 1))
+            quantize(
+                w1_mx[0][:, columns],
+                w1_mx[1][:, columns],
+                w1_grouped[:, 2 * pair : 2 * pair + 2, :, :].rearrange("p t m j -> p (t m j)"),
+            )
+        nc.vector.tensor_copy(picked[0][:], word_table[:].indirect(offs_tile[:]))
+
+        y_bank = [psum.tile([P, S], F32, name="y_bank%d" % t, tag="bank%d" % t) for t in range(PACK)]
         for t in range(PACK):
-            nc.vector.tensor_tensor(max_a[:, t, :], y3[:, t, :], y_rows[t][:, :S], ALU.max)
-            nc.vector.tensor_tensor(max_b[:, t, :], y4[:, t, :], y5[:, t, :], ALU.max)
-        w2_codes = keep.tile([P, N], U32, align_bytes=64)
-        w2_scales = keep.tile([P, N], U8, align_bytes=64)
-        nc.vector.quantize_mx(w2_codes[:].bitcast(FP8X4), w2_scales[:], w2_bf[:].rearrange("p c j -> p (c j)"))
-        nc.vector.tensor_tensor(diff[:], max_a[:], max_b[:], ALU.subtract)
+            product(y_bank[t][:], t, w1_mx, picked)
+        nc.vector.tensor_copy(candidates[0][:], word_table[:].indirect(cand_tile[:]))
+        nc.scalar.copy(y_rows[0][:, :S], y_bank[0][:])
+        for t in range(1, PACK):
+            nc.vector.tensor_copy(y_rows[t][:, :S], y_bank[t][:])
 
-        squares = keep.tile([P, 2, PACK, S], F32)
-        nc.scalar.activation(squares[:], ev[:], ACT.Square)
-
-        z2_bf = keep.tile([P, S, PACK], BF16, align_bytes=64)
-        nc.vector.tensor_tensor(
-            z2_bf[:].rearrange("p (c i) t -> p c t i", i=4),
-            diff[:].rearrange("p t (c i) -> p c t i", i=4),
-            gs_t[:].unsqueeze(1).unsqueeze(3).broadcast_to([P, S // 4, PACK, 4]),
-            ALU.mult,
-        )
-        spread = keep.tile([P, PACK, S], F32)
-        nc.vector.scalar_tensor_tensor(spread[:], squares[:, 0, :, :], 0.140625, squares[:, 1, :, :], ALU.mult, ALU.add)
-        z2_codes = keep.tile([P, S], U32, align_bytes=64)
-        z2_scales = keep.tile([P, S], U8, align_bytes=64)
-        nc.vector.quantize_mx(z2_codes[:].bitcast(FP8X4), z2_scales[:], z2_bf[:].rearrange("p j t -> p (j t)"))
-
-        inv = keep.tile([P, PACK, S], F32)
-        nc.scalar.activation(inv[:], spread[:], ACT.Abs_reciprocal_sqrt, bias=2.56, scale=5.12)
-
-        b_psum = [psum.tile([P, 2, S], F32, name="b_psum%d" % h) for h in range(2)]
-        for r in range(4):
-            cols = slice(P * r, P * (r + 1))
-            mx(b_psum[r // 2][:, r % 2, :], cand_words[:, cols], cand_scales[:, cols], z2_codes[:], z2_scales[:])
-        b6 = keep.tile([P, 4, S], F32)
-        for r in range(4):
-            nc.scalar.copy(b_rows[r][:, :S], b_psum[r // 2][:, r % 2, :])
-            nc.scalar.activation(b6[:, r, :], b_rows[r][:].indirect(n6_t[:]), ACT.Copy)
-
-        z = keep.tile([P, PACK, S], F32)
+        minus_pa, u, y_scaled = four_tiles("minus_pa"), four_tiles("u"), four_tiles("y_scaled")
+        sums = []
         for t in range(PACK):
-            nc.vector.scalar_tensor_tensor(z[:, t, :], centred[:, t, :], gn_t[:, t : t + 1], inv[:, t, :], ALU.mult, ALU.mult)
-        z_bf = keep.tile([P, S, PACK], BF16, align_bytes=64)
-        nc.vector.tensor_copy(
-            z_bf[:].rearrange("p (c i) t -> p c t i", i=4), z[:].rearrange("p t (c i) -> p c t i", i=4)
-        )
-        b_diff = keep.tile([P, 4, S], F32)
-        nc.vector.tensor_tensor(b_diff[:, 0, :], b_rows[0][:].indirect(n7_t[:]), b6[:, 0, :], ALU.subtract)
-        z_codes = keep.tile([P, S], U32, align_bytes=64)
-        z_scales = keep.tile([P, S], U8, align_bytes=64)
-        nc.vector.quantize_mx(z_codes[:].bitcast(FP8X4), z_scales[:], z_bf[:].rearrange("p j t -> p (j t)"))
-        a_psum = [psum.tile([P, 2, S], F32, name="a_psum%d" % h) for h in range(2)]
-        for r in range(4):
-            cols = slice(P * r, P * (r + 1))
-            mx(a_psum[r // 2][:, r % 2, :], w2_codes[:, cols], w2_scales[:, cols], z_codes[:], z_scales[:])
-        for r in range(1, 4):
-            nc.vector.tensor_tensor(b_diff[:, r, :], b_rows[r][:].indirect(n7_t[:]), b6[:, r, :], ALU.subtract)
+            fetch(minus_pa[:, t, :], y_rows[t], n1_tile, scale=-1.0)
+            nc.vector.tensor_scalar(y_scaled[:, t, :], y_rows[t][:, :S], -5.0 / 3.0, None, ALU.mult)
+            nc.vector.tensor_tensor(u[:, t, :], y_rows[t][:].indirect(n2_tile[:]), minus_pa[:, t, :], ALU.subtract)
+            sums.append(psum.tile([P, 2, HALVES, P], F32, name="sums%d" % t, tag="bank%d" % t))
+            for h in range(HALVES):
+                columns = slice(P * h, P * (h + 1))
+                transposed_sum(sums[t][:, 0, h, :], [u[:, t, columns], y_scaled[:, t, columns]])
+                transposed_sum(
+                    sums[t][:, 1, h, :], [u[:, t, columns], minus_pa[:, t, columns], minus_pa[:, t, columns]]
+                )
 
-        gate = keep.tile([P, 4, S], F32)
-        result = keep.tile([P, 4, S], F32)
-        for r in range(4):
-            nc.scalar.activation(gate[:, r, :], b_diff[:, r, :], ACT.Tanh, scale=-0.0625)
-        for r in range(4):
-            nc.vector.tensor_tensor(result[:, r, :], a_psum[r // 2][:, r % 2, :], gate[:, r, :], ALU.mult)
+        w2_grouped = keep.tile([P, N, PACK], BF16, align_bytes=64)
+        w2_mx = mx_operand("w2_mx", N)
+        interleave(w2_grouped, w2_rows)
+
+        y3, y4, y5 = four_tiles("y3"), four_tiles("y4"), four_tiles("y5")
+        max_y3, max_45, gs_max_45, z2 = [four_tiles(s) for s in ("max_y3", "max_45", "gs_max_45", "z2")]
+
+        def difference(t):
+            nc.vector.scalar_tensor_tensor(
+                z2[:, t, :], max_y3[:, t, :], gs_tile[:, t : t + 1], gs_max_45[:, t, :], ALU.mult, ALU.subtract
+            )
+
+        for t in range(PACK):
+            fetch(y4[:, t, :], y_rows[t], n4_tile)
+            fetch(y5[:, t, :], y_rows[t], n5_tile)
+            fetch(y3[:, t, :], y_rows[t], n3_tile)
+            if t == PACK - 1:
+                quantize(w2_mx[0][:], w2_mx[1][:], w2_grouped[:].rearrange("p c j -> p (c j)"))
+            nc.vector.tensor_tensor(max_45[:, t, :], y4[:, t, :], y5[:, t, :], ALU.max)
+            if t > 0:
+                difference(t - 1)
+            nc.vector.tensor_tensor(max_y3[:, t, :], y_rows[t][:, :S], y3[:, t, :], ALU.max)
+            nc.vector.tensor_scalar(gs_max_45[:, t, :], max_45[:, t, :], gs_tile[:, t : t + 1], None, ALU.mult)
+
+        squares = keep.tile([P, PACK, 2, HALVES, P], F32)
+        inverse_root = four_tiles("inverse_root")
+        square_sum = []
+        for t in range(PACK):
+            nc.scalar.activation(squares[:, t, 0, :, :], sums[t][:, 0, :, :], ACT.Square, scale=0.375)
+            nc.scalar.activation(squares[:, t, 1, :, :], sums[t][:, 1, :, :], ACT.Square)
+            square_sum.append(psum.tile([P, S], F32, name="square_sum%d" % t, tag="bank%d" % t))
+            for kind in range(2):
+                for h in range(HALVES):
+                    nc.tensor.matmul(
+                        square_sum[t][:, P * h : P * (h + 1)],
+                        squares[:, t, kind, h, :],
+                        identity[:],
+                        start=(kind == 0 and h == 0),
+                        stop=(kind == 1 and h == HALVES - 1),
+                        is_transpose=True,
+                    )
+        for t in range(PACK):
+            nc.scalar.activation(
+                inverse_root[:, t, :], square_sum[t][:], ACT.Abs_reciprocal_sqrt, bias=ROOT_BIAS, scale=ROOT_SCALE
+            )
+
+        warm_tanh = keep.tile([P, 1], F32)
+        nc.scalar.activation(warm_tanh[:], inverse_root[:, PACK - 1, 0:1], ACT.Tanh)
+
+        centred = four_tiles("centred")
+        z2_grouped = keep.tile([P, S, PACK], BF16, align_bytes=64)
+        z2_mx = mx_operand("z2_mx", S)
+
+        def centre(t):
+            nc.vector.scalar_tensor_tensor(
+                centred[:, t, :], y_rows[t][:, :S], 2.2, u[:, t, :], ALU.mult, ALU.subtract
+            )
+
+        centre(0)
+        difference(PACK - 1)
+        centre(1)
+        interleave(z2_grouped, z2)
+        centre(2)
+        quantize(z2_mx[0][:], z2_mx[1][:], z2_grouped[:].rearrange("p c t -> p (c t)"))
+        centre(3)
+
+        b_bank = [psum.tile([P, 2, S], F32, name="b_bank%d" % i) for i in range(BLOCKS // 2)]
+        a_bank = [psum.tile([P, 2, S], F32, name="a_bank%d" % i) for i in range(BLOCKS // 2)]
+        for r in range(BLOCKS):
+            product(b_bank[r // 2][:, r % 2, :], r, candidates, z2_mx)
+
+        z = four_tiles("z")
+        for t in range(PACK):
+            nc.vector.scalar_tensor_tensor(
+                z[:, t, :], centred[:, t, :], gn_tile[:, t : t + 1], inverse_root[:, t, :], ALU.mult, ALU.mult
+            )
+
+        def empty_b_bank(i):
+            for r in (2 * i, 2 * i + 1):
+                nc.vector.tensor_copy(b_rows[r][:, :S], b_bank[i][:, r % 2, :])
+
+        z_grouped = keep.tile([P, S, PACK], BF16, align_bytes=64)
+        z_mx = mx_operand("z_mx", S)
+        empty_b_bank(0)
+        interleave(z_grouped, z)
+        empty_b_bank(1)
+        quantize(z_mx[0][:], z_mx[1][:], z_grouped[:].rearrange("p c t -> p (c t)"))
+        for r in range(BLOCKS):
+            product(a_bank[r // 2][:, r % 2, :], r, w2_mx, z_mx)
+
+        b6, b7_less_b6, gate, result = [four_tiles(s) for s in ("b6", "b7_less_b6", "gate", "result")]
+        for r in range(BLOCKS):
+            fetch(b6[:, r, :], b_rows[r], n6_tile)
+        for r in range(BLOCKS):
+            nc.vector.tensor_tensor(b7_less_b6[:, r, :], b_rows[r][:].indirect(n7_tile[:]), b6[:, r, :], ALU.subtract)
+        for r in range(BLOCKS):
+            nc.scalar.activation(gate[:, r, :], b7_less_b6[:, r, :], ACT.Tanh, scale=-0.0625)
+        for r in range(BLOCKS):
+            nc.vector.tensor_tensor(result[:, r, :], a_bank[r // 2][:, r % 2, :], gate[:, r, :], ALU.mult)
             nc.sync.dma_start(out[P * r : P * (r + 1), :], result[:, r, :])

from contextlib import ExitStack

import concourse.mybir as mybir
from concourse.masks import make_identity

K, T, S, N, H, C = 512, 2048, 256, 512, 512, 512
FLOPS = 2 * K * H * S + 2 * H * N * S + 2 * K * C * S

F32 = mybir.dt.float32
BF16 = mybir.dt.bfloat16
I32 = mybir.dt.int32
U32 = mybir.dt.uint32
U16 = mybir.dt.uint16
U8 = mybir.dt.uint8
FP8X4 = mybir.dt.float8_e4m3fn_x4
ALU = mybir.AluOpType
ACT = mybir.ActivationFunctionType

P = 128
PACK = 4
BLOCKS = N // P
HALVES = S // P
WINDOW = 2 * S
RUN = 4

ROOT_SCALE = 0.5 / 0.3125**2
ROOT_BIAS = 0.25 / 0.3125**2


def tile_picked_fkcdjointbstdmix_none_p_kernel(
    tc, x_words, x_scales, w1, gn, w2, gs, offs, n1, n2, n3, n4, n5, cand, n6, n7, out
):
    nc = tc.nc
    with ExitStack() as ctx:
        keep = ctx.enter_context(tc.tile_pool(name="keep", bufs=1))
        psum = ctx.enter_context(tc.psum_pool(name="psum", bufs=1))

        def load_list(name, source):
            tile = keep.tile(list(source.shape), U16, name=name)
            nc.sync.dma_start(tile[:], source)
            return tile

        def four_tiles(name):
            return keep.tile([P, PACK, S], F32, name=name)

        def mx_operand(name, columns):
            words = keep.tile([P, columns], U32, name=name + "_words", align_bytes=64)
            scales = keep.tile([P, columns], U8, name=name + "_scales", align_bytes=64)
            return words, scales

        def interleave(grouped, tiles):
            nc.vector.tensor_copy(
                grouped[:].rearrange("p (c i) t -> p c t i", i=RUN),
                tiles[:].rearrange("p t (c i) -> p c t i", i=RUN),
            )

        def quantize(words, scales, grouped):
            nc.vector.quantize_mx(words.bitcast(FP8X4), scales, grouped)

        def product(result, block, stationary, moving):
            columns = slice(P * block, P * (block + 1))
            nc.tensor.matmul_mx(
                out=result,
                lhsT=stationary[0][:, columns].bitcast(FP8X4),
                lhsT_scale=stationary[1][:, columns],
                rhs=moving[0][:].bitcast(FP8X4),
                rhs_scale=moving[1][:],
                start=True,
                stop=True,
            )

        def transposed_sum(result, terms):
            for i, term in enumerate(terms):
                nc.tensor.matmul(
                    result, term, identity[:], start=(i == 0), stop=(i == len(terms) - 1), is_transpose=True
                )

        def fetch(result, rows, offsets, scale=1.0):
            nc.scalar.activation(result, rows[:].indirect(offsets[:]), ACT.Copy, scale=scale)

        identity = keep.tile([P, P], F32)
        make_identity(nc, identity[:])

        gs_tile = keep.tile([P, PACK], F32)
        nc.gpsimd.dma_start(gs_tile[:], gs.rearrange("(p t) o -> p (t o)", t=PACK))
        gn_tile = keep.tile([P, PACK], F32)
        nc.gpsimd.dma_start(gn_tile[:], gn.rearrange("(p t) o -> p (t o)", t=PACK))

        scale_table = keep.tile([P, T], U8, align_bytes=64)
        nc.vector.memset(scale_table[:].bitcast(I32), 0)
        y_rows = [keep.tile([P, WINDOW], F32, name="y_rows%d" % t) for t in range(PACK)]
        b_rows = [keep.tile([P, WINDOW], F32, name="b_rows%d" % r) for r in range(BLOCKS)]
        for rows in y_rows + b_rows:
            nc.vector.memset(rows[:, S:], 0.0)

        warm_root = keep.tile([P, 1], F32)
        nc.scalar.activation(
            warm_root[:], y_rows[0][:, S : S + 1], ACT.Abs_reciprocal_sqrt, bias=ROOT_BIAS, scale=ROOT_SCALE
        )

        offs_tile = load_list("offs_tile", offs)
        cand_tile = load_list("cand_tile", cand)
        w1_rows = w1.rearrange("(p j) c -> p j c", j=PACK)
        w1_low = keep.tile([P, PACK, H // 2], F32)
        nc.sync.dma_start(w1_low[:], w1_rows[:, :, : H // 2])
        for quadrant in range(4):
            nc.sync.dma_start(
                scale_table[32 * quadrant : 32 * quadrant + 4, :].bitcast(I32),
                x_scales[0, 4 * quadrant : 4 * quadrant + 4, :].bitcast(I32),
            )
        w1_high = keep.tile([P, PACK, H // 2], F32)
        nc.sync.dma_start(w1_high[:], w1_rows[:, :, H // 2 :])
        word_table = keep.tile([P, T], U32, align_bytes=64)
        nc.sync.dma_start(word_table[:].bitcast(I32), x_words[0].rearrange("p c r -> p (c r)").bitcast(I32))
        n1_tile = load_list("n1_tile", n1)
        n2_tile = load_list("n2_tile", n2)
        n4_tile = load_list("n4_tile", n4)
        n5_tile = load_list("n5_tile", n5)
        n3_tile = load_list("n3_tile", n3)
        w2_rows = keep.tile([P, PACK, N], F32)
        nc.sync.dma_start(w2_rows[:], w2.rearrange("(p j) c -> p j c", j=PACK))
        n6_tile = load_list("n6_tile", n6)
        n7_tile = load_list("n7_tile", n7)

        picked = mx_operand("picked", S)
        candidates = mx_operand("candidates", C)
        w1_mx = mx_operand("w1_mx", H)
        w1_grouped = keep.tile([P, PACK, P, PACK], BF16, align_bytes=64)

        def dealt(first, last):
            return w1_grouped[:, :, first:last, :].rearrange("p t m j -> p m j t")

        def by_channel(columns):
            return columns.rearrange("p j (m t) -> p m j t", t=PACK)

        nc.scalar.activation(dealt(0, P // 2), by_channel(w1_low[:]), ACT.Copy)
        nc.vector.tensor_copy(picked[1][:], scale_table[:].indirect(offs_tile[:]))
        nc.vector.tensor_copy(candidates[1][:], scale_table[:].indirect(cand_tile[:]))
        nc.vector.tensor_copy(dealt(P // 2, 3 * P // 4), by_channel(w1_high[:, :, : H // 4]))
        nc.scalar.activation(dealt(3 * P // 4, P), by_channel(w1_high[:, :, H // 4 :]), ACT.Copy)
        for pair in range(PACK // 2):
            columns = slice(2 * P * pair, 2 * P * (pair + 1))
            quantize(
                w1_mx[0][:, columns],
                w1_mx[1][:, columns],
                w1_grouped[:, 2 * pair : 2 * pair + 2, :, :].rearrange("p t m j -> p (t m j)"),
            )
        nc.vector.tensor_copy(picked[0][:], word_table[:].indirect(offs_tile[:]))

        y_bank = [psum.tile([P, S], F32, name="y_bank%d" % t, tag="bank%d" % t) for t in range(PACK)]
        for t in range(PACK):
            product(y_bank[t][:], t, w1_mx, picked)
        nc.vector.tensor_copy(candidates[0][:], word_table[:].indirect(cand_tile[:]))
        nc.scalar.copy(y_rows[0][:, :S], y_bank[0][:])
        for t in range(1, PACK):
            nc.vector.tensor_copy(y_rows[t][:, :S], y_bank[t][:])

        minus_pa, u, y_scaled = four_tiles("minus_pa"), four_tiles("u"), four_tiles("y_scaled")
        sums = []
        for t in range(PACK):
            fetch(minus_pa[:, t, :], y_rows[t], n1_tile, scale=-1.0)
            nc.vector.tensor_scalar(y_scaled[:, t, :], y_rows[t][:, :S], -5.0 / 3.0, None, ALU.mult)
            nc.vector.tensor_tensor(u[:, t, :], y_rows[t][:].indirect(n2_tile[:]), minus_pa[:, t, :], ALU.subtract)
            sums.append(psum.tile([P, 2, HALVES, P], F32, name="sums%d" % t, tag="bank%d" % t))
            for h in range(HALVES):
                columns = slice(P * h, P * (h + 1))
                transposed_sum(sums[t][:, 0, h, :], [u[:, t, columns], y_scaled[:, t, columns]])
                transposed_sum(
                    sums[t][:, 1, h, :], [u[:, t, columns], minus_pa[:, t, columns], minus_pa[:, t, columns]]
                )

        w2_grouped = keep.tile([P, N, PACK], BF16, align_bytes=64)
        w2_mx = mx_operand("w2_mx", N)
        interleave(w2_grouped, w2_rows)

        y3, y4, y5 = four_tiles("y3"), four_tiles("y4"), four_tiles("y5")
        max_y3, max_45, gs_max_45, z2 = [four_tiles(s) for s in ("max_y3", "max_45", "gs_max_45", "z2")]

        def difference(t):
            nc.vector.scalar_tensor_tensor(
                z2[:, t, :], max_y3[:, t, :], gs_tile[:, t : t + 1], gs_max_45[:, t, :], ALU.mult, ALU.subtract
            )

        for t in range(PACK):
            fetch(y4[:, t, :], y_rows[t], n4_tile)
            fetch(y5[:, t, :], y_rows[t], n5_tile)
            fetch(y3[:, t, :], y_rows[t], n3_tile)
            if t == PACK - 1:
                quantize(w2_mx[0][:], w2_mx[1][:], w2_grouped[:].rearrange("p c j -> p (c j)"))
            nc.vector.tensor_tensor(max_45[:, t, :], y4[:, t, :], y5[:, t, :], ALU.max)
            if t > 0:
                difference(t - 1)
            nc.vector.tensor_tensor(max_y3[:, t, :], y_rows[t][:, :S], y3[:, t, :], ALU.max)
            nc.vector.tensor_scalar(gs_max_45[:, t, :], max_45[:, t, :], gs_tile[:, t : t + 1], None, ALU.mult)

        squares = keep.tile([P, PACK, 2, HALVES, P], F32)
        inverse_root = four_tiles("inverse_root")
        square_sum = []
        for t in range(PACK):
            nc.scalar.activation(squares[:, t, 0, :, :], sums[t][:, 0, :, :], ACT.Square, scale=0.375)
            nc.scalar.activation(squares[:, t, 1, :, :], sums[t][:, 1, :, :], ACT.Square)
            square_sum.append(psum.tile([P, S], F32, name="square_sum%d" % t, tag="bank%d" % t))
            for kind in range(2):
                for h in range(HALVES):
                    nc.tensor.matmul(
                        square_sum[t][:, P * h : P * (h + 1)],
                        squares[:, t, kind, h, :],
                        identity[:],
                        start=(kind == 0 and h == 0),
                        stop=(kind == 1 and h == HALVES - 1),
                        is_transpose=True,
                    )
        for t in range(PACK):
            nc.scalar.activation(
                inverse_root[:, t, :], square_sum[t][:], ACT.Abs_reciprocal_sqrt, bias=ROOT_BIAS, scale=ROOT_SCALE
            )

        warm_tanh = keep.tile([P, 1], F32)
        nc.scalar.activation(warm_tanh[:], inverse_root[:, PACK - 1, 0:1], ACT.Tanh)

        centred = four_tiles("centred")
        z2_grouped = keep.tile([P, S, PACK], BF16, align_bytes=64)
        z2_mx = mx_operand("z2_mx", S)

        def centre(t):
            nc.vector.scalar_tensor_tensor(
                centred[:, t, :], y_rows[t][:, :S], 2.2, u[:, t, :], ALU.mult, ALU.subtract
            )

        centre(0)
        difference(PACK - 1)
        centre(1)
        interleave(z2_grouped, z2)
        centre(2)
        quantize(z2_mx[0][:], z2_mx[1][:], z2_grouped[:].rearrange("p c t -> p (c t)"))
        centre(3)

        b_bank = [psum.tile([P, 2, S], F32, name="b_bank%d" % i) for i in range(BLOCKS // 2)]
        a_bank = [psum.tile([P, 2, S], F32, name="a_bank%d" % i) for i in range(BLOCKS // 2)]
        for r in range(BLOCKS):
            product(b_bank[r // 2][:, r % 2, :], r, candidates, z2_mx)

        z = four_tiles("z")
        for t in range(PACK):
            nc.vector.scalar_tensor_tensor(
                z[:, t, :], centred[:, t, :], gn_tile[:, t : t + 1], inverse_root[:, t, :], ALU.mult, ALU.mult
            )

        def empty_b_bank(i):
            for r in (2 * i, 2 * i + 1):
                nc.vector.tensor_copy(b_rows[r][:, :S], b_bank[i][:, r % 2, :])

        z_grouped = keep.tile([P, S, PACK], BF16, align_bytes=64)
        z_mx = mx_operand("z_mx", S)
        empty_b_bank(0)
        interleave(z_grouped, z)
        empty_b_bank(1)
        quantize(z_mx[0][:], z_mx[1][:], z_grouped[:].rearrange("p c t -> p (c t)"))
        for r in range(BLOCKS):
            product(a_bank[r // 2][:, r % 2, :], r, w2_mx, z_mx)

        b6, b7_less_b6, gate, result = [four_tiles(s) for s in ("b6", "b7_less_b6", "gate", "result")]
        for r in range(BLOCKS):
            fetch(b6[:, r, :], b_rows[r], n6_tile)
        for r in range(BLOCKS):
            nc.vector.tensor_tensor(b7_less_b6[:, r, :], b_rows[r][:].indirect(n7_tile[:]), b6[:, r, :], ALU.subtract)
        for r in range(BLOCKS):
            nc.scalar.activation(gate[:, r, :], b7_less_b6[:, r, :], ACT.Tanh, scale=-0.0625)
        for r in range(BLOCKS):
            nc.vector.tensor_tensor(result[:, r, :], a_bank[r // 2][:, r % 2, :], gate[:, r, :], ALU.mult)
            nc.sync.dma_start(out[P * r : P * (r + 1), :], result[:, r, :])
